import numpy as np
import ml_dtypes

BF16 = ml_dtypes.bfloat16


def bf(x):
    return np.asarray(x, np.float32).astype(BF16)


def f32(x):
    return np.asarray(x, np.float32)


def f64(x):
    return np.asarray(x).astype(np.float64)


def striped(idx):
    return np.concatenate([l.reshape(-1, 16).T for l in idx])


def rows(idx, k):
    return np.tile(np.repeat(idx, 16, axis=0), (k // (16 * 8), 1))


def look(tab, idx):
    return np.take_along_axis(f64(tab), rows(idx, len(tab)), axis=1)


K, S, V, N, M = 256, 2048, 1024, 1024, 256


def setup_inputs():
    return {"tab": f32(np.random.standard_normal((K, S))), "y": f32(np.random.standard_normal((K, V))), "w": bf(np.random.standard_normal((K, M)) / np.sqrt(K)), "offs": striped(np.stack([np.random.permutation(S)[:N] for _ in range(8)]))}


def reference(tab, y, w, offs):
    idx = np.stack([g.T.reshape(-1) for g in np.split(offs, 8)])
    t = look(tab, idx)
    x = t**2 * f64(y)
    y = f64(w).T @ x
    return y

@@ -1,0 +1,73 @@
+import concourse.mybir as mybir
+
+BF16, F32, U16 = mybir.dt.bfloat16, mybir.dt.float32, mybir.dt.uint16
+MULT = mybir.AluOpType.mult
+SQUARE = mybir.ActivationFunctionType.Square
+
+P = 128
+K, S, N, M = 256, 2048, 1024, 256
+BLOCKS = K // P
+PIECE = 512
+PIECES = N // PIECE
+OUT_BLOCKS = M // P
+
+FLOPS = 2 * K * M * N
+
+
+def tile_lookup_gate_sq_none_kernel(tc, tab, y, w, offs, out):
+    nc = tc.nc
+    with (
+        tc.tile_pool(name="held", bufs=1) as held,
+        tc.psum_pool(name="psum", bufs=1) as psum,
+    ):
+        lists = held.tile([P, N // 16], U16, name="lists")
+        nc.sync.dma_start(lists[:], offs)
+
+        tables = []
+        for b in range(BLOCKS):
+            table = held.tile([P, S], F32, name=f"table{b}")
+            nc.sync.dma_start(table[:], tab[b * P : (b + 1) * P, :])
+            tables.append(table)
+
+        weights = held.tile([P, BLOCKS, M], BF16, name="weights")
+        nc.sync.dma_start(weights[:], w.rearrange("(b p) m -> p b m", p=P))
+
+        streams = {}
+        for b in range(BLOCKS):
+            for c in range(PIECES):
+                stream = held.tile([P, PIECE], F32, name=f"stream{b}{c}")
+                nc.sync.dma_start(stream[:], y[b * P : (b + 1) * P, c * PIECE : (c + 1) * PIECE])
+                streams[b, c] = stream
+
+        sums = {
+            (m, c): psum.tile([P, PIECE], F32, name=f"sum{m}{c}")
+            for c in range(PIECES)
+            for m in range(OUT_BLOCKS)
+        }
+
+        for b in range(BLOCKS):
+            for c in range(PIECES):
+                squares = held.tile([P, PIECE], F32, name=f"squares{b}{c}")
+                piece = lists[:, c * PIECE // 16 : (c + 1) * PIECE // 16]
+                nc.scalar.activation(squares[:], tables[b][:].indirect(piece), SQUARE)
+
+                x = held.tile([P, PIECE], BF16, name=f"x{b}{c}")
+                nc.vector.tensor_tensor(x[:], squares[:], streams[b, c][:], MULT)
+
+                for m in range(OUT_BLOCKS):
+                    nc.tensor.matmul(
+                        sums[m, c][:],
+                        weights[:, b, m * P : (m + 1) * P],
+                        x[:],
+                        start=b == 0,
+                        stop=b == BLOCKS - 1,
+                    )
+
+        for c in range(PIECES):
+            for m in range(OUT_BLOCKS):
+                result = held.tile([P, PIECE], F32, name=f"result{m}{c}")
+                if m == 0:
+                    nc.scalar.copy(result[:], sums[m, c][:])
+                else:
+                    nc.vector.tensor_copy(result[:], sums[m, c][:])
+                nc.sync.dma_start(out[m * P : (m + 1) * P, c * PIECE : (c + 1) * PIECE], result[:])

@@ -20,24 +20,35 @@ def tile_lookup_gate_sq_none_kernel(tc, tab, y, w, offs, out):
         tc.tile_pool(name="held", bufs=1) as held,
         tc.psum_pool(name="psum", bufs=1) as psum,
     ):
+        warm_in = held.tile([P, 1], F32, name="warm_in")
+        nc.vector.memset(warm_in[:], 0.0)
+        warm_out = held.tile([P, 1], F32, name="warm_out")
+        nc.scalar.activation(warm_out[:], warm_in[:], SQUARE)
+
         lists = held.tile([P, N // 16], U16, name="lists")
         nc.sync.dma_start(lists[:], offs)
 
-        tables = []
+        tables, streams = [], {}
         for b in range(BLOCKS):
             table = held.tile([P, S], F32, name=f"table{b}")
-            nc.sync.dma_start(table[:], tab[b * P : (b + 1) * P, :])
             tables.append(table)
-
-        weights = held.tile([P, BLOCKS, M], BF16, name="weights")
-        nc.sync.dma_start(weights[:], w.rearrange("(b p) m -> p b m", p=P))
-
-        streams = {}
-        for b in range(BLOCKS):
             for c in range(PIECES):
-                stream = held.tile([P, PIECE], F32, name=f"stream{b}{c}")
-                nc.sync.dma_start(stream[:], y[b * P : (b + 1) * P, c * PIECE : (c + 1) * PIECE])
-                streams[b, c] = stream
+                streams[b, c] = held.tile([P, PIECE], F32, name=f"stream{b}{c}")
+        weights = held.tile([P, BLOCKS, M], BF16, name="weights")
+
+        def load_table(b):
+            nc.sync.dma_start(tables[b][:], tab[b * P : (b + 1) * P, :])
+
+        def load_stream(b, c):
+            nc.sync.dma_start(streams[b, c][:], y[b * P : (b + 1) * P, c * PIECE : (c + 1) * PIECE])
+
+        load_table(0)
+        nc.sync.dma_start(weights[:], w.rearrange("(b p) m -> p b m", p=P))
+        load_stream(0, 0)
+        load_table(1)
+        load_stream(0, 1)
+        load_stream(1, 0)
+        load_stream(1, 1)
 
         sums = {
             (m, c): psum.tile([P, PIECE], F32, name=f"sum{m}{c}")
@@ -45,14 +56,18 @@ def tile_lookup_gate_sq_none_kernel(tc, tab, y, w, offs, out):
             for m in range(OUT_BLOCKS)
         }
 
+        squares = {}
         for b in range(BLOCKS):
             for c in range(PIECES):
-                squares = held.tile([P, PIECE], F32, name=f"squares{b}{c}")
+                square = held.tile([P, PIECE], F32, name=f"square{b}{c}")
                 piece = lists[:, c * PIECE // 16 : (c + 1) * PIECE // 16]
-                nc.scalar.activation(squares[:], tables[b][:].indirect(piece), SQUARE)
+                nc.scalar.activation(square[:], tables[b][:].indirect(piece), SQUARE)
+                squares[b, c] = square
 
+        for b in range(BLOCKS):
+            for c in range(PIECES):
                 x = held.tile([P, PIECE], BF16, name=f"x{b}{c}")
-                nc.vector.tensor_tensor(x[:], squares[:], streams[b, c][:], MULT)
+                nc.vector.tensor_tensor(x[:], squares[b, c][:], streams[b, c][:], MULT)
 
                 for m in range(OUT_BLOCKS):
                     nc.tensor.matmul(
@@ -63,11 +78,11 @@ def tile_lookup_gate_sq_none_kernel(tc, tab, y, w, offs, out):
                         stop=b == BLOCKS - 1,
                     )
 
-        for c in range(PIECES):
-            for m in range(OUT_BLOCKS):
-                result = held.tile([P, PIECE], F32, name=f"result{m}{c}")
-                if m == 0:
-                    nc.scalar.copy(result[:], sums[m, c][:])
-                else:
-                    nc.vector.tensor_copy(result[:], sums[m, c][:])
-                nc.sync.dma_start(out[m * P : (m + 1) * P, c * PIECE : (c + 1) * PIECE], result[:])
+                if b == BLOCKS - 1:
+                    for m in range(OUT_BLOCKS):
+                        result = held.tile([P, PIECE], F32, name=f"result{m}{c}")
+                        if m == 0:
+                            nc.vector.tensor_copy(result[:], sums[m, c][:])
+                        else:
+                            nc.scalar.copy(result[:], sums[m, c][:])
+                        nc.sync.dma_start(out[m * P : (m + 1) * P, c * PIECE : (c + 1) * PIECE], result[:])

@@ -7,9 +7,11 @@ SQUARE = mybir.ActivationFunctionType.Square
 P = 128
 K, S, N, M = 256, 2048, 1024, 256
 BLOCKS = K // P
+OUT_BLOCKS = M // P
 PIECE = 512
 PIECES = N // PIECE
-OUT_BLOCKS = M // P
+PART = PIECE // 2
+PARTS = PIECE // PART
 
 FLOPS = 2 * K * M * N
 
@@ -20,21 +22,18 @@ def tile_lookup_gate_sq_none_kernel(tc, tab, y, w, offs, out):
         tc.tile_pool(name="held", bufs=1) as held,
         tc.psum_pool(name="psum", bufs=1) as psum,
     ):
-        warm_in = held.tile([P, 1], F32, name="warm_in")
-        nc.vector.memset(warm_in[:], 0.0)
-        warm_out = held.tile([P, 1], F32, name="warm_out")
-        nc.scalar.activation(warm_out[:], warm_in[:], SQUARE)
+        early_in = held.tile([P, 1], F32, name="early_in")
+        nc.vector.memset(early_in[:], 0.0)
+        early_out = held.tile([P, 1], F32, name="early_out")
+        nc.scalar.activation(early_out[:], early_in[:], SQUARE)
 
         lists = held.tile([P, N // 16], U16, name="lists")
-        nc.sync.dma_start(lists[:], offs)
-
-        tables, streams = [], {}
+        weights = held.tile([P, BLOCKS, M], BF16, name="weights")
+        tables, streams = {}, {}
         for b in range(BLOCKS):
-            table = held.tile([P, S], F32, name=f"table{b}")
-            tables.append(table)
+            tables[b] = held.tile([P, S], F32, name=f"table{b}")
             for c in range(PIECES):
                 streams[b, c] = held.tile([P, PIECE], F32, name=f"stream{b}{c}")
-        weights = held.tile([P, BLOCKS, M], BF16, name="weights")
 
         def load_table(b):
             nc.sync.dma_start(tables[b][:], tab[b * P : (b + 1) * P, :])
@@ -43,6 +42,7 @@ def tile_lookup_gate_sq_none_kernel(tc, tab, y, w, offs, out):
             nc.sync.dma_start(streams[b, c][:], y[b * P : (b + 1) * P, c * PIECE : (c + 1) * PIECE])
 
         load_table(0)
+        nc.sync.dma_start(lists[:], offs)
         nc.sync.dma_start(weights[:], w.rearrange("(b p) m -> p b m", p=P))
         load_stream(0, 0)
         load_table(1)
@@ -50,39 +50,43 @@ def tile_lookup_gate_sq_none_kernel(tc, tab, y, w, offs, out):
         load_stream(1, 0)
         load_stream(1, 1)
 
-        sums = {
-            (m, c): psum.tile([P, PIECE], F32, name=f"sum{m}{c}")
-            for c in range(PIECES)
-            for m in range(OUT_BLOCKS)
-        }
-
         squares = {}
         for b in range(BLOCKS):
             for c in range(PIECES):
-                square = held.tile([P, PIECE], F32, name=f"square{b}{c}")
+                squares[b, c] = held.tile([P, PIECE], F32, name=f"square{b}{c}")
                 piece = lists[:, c * PIECE // 16 : (c + 1) * PIECE // 16]
-                nc.scalar.activation(square[:], tables[b][:].indirect(piece), SQUARE)
-                squares[b, c] = square
+                nc.scalar.activation(squares[b, c][:], tables[b][:].indirect(piece), SQUARE)
+
+        sums = {
+            (m, c, h): psum.tile([P, PART], F32, name=f"sum{m}{c}{h}")
+            for m in range(OUT_BLOCKS)
+            for c in range(PIECES)
+            for h in range(PARTS)
+        }
 
         for b in range(BLOCKS):
             for c in range(PIECES):
-                x = held.tile([P, PIECE], BF16, name=f"x{b}{c}")
-                nc.vector.tensor_tensor(x[:], squares[b, c][:], streams[b, c][:], MULT)
+                for h in range(PARTS):
+                    part = slice(h * PART, (h + 1) * PART)
+                    x = held.tile([P, PART], BF16, name=f"x{b}{c}{h}")
+                    nc.vector.tensor_tensor(x[:], squares[b, c][:, part], streams[b, c][:, part], MULT)
 
-                for m in range(OUT_BLOCKS):
-                    nc.tensor.matmul(
-                        sums[m, c][:],
-                        weights[:, b, m * P : (m + 1) * P],
-                        x[:],
-                        start=b == 0,
-                        stop=b == BLOCKS - 1,
-                    )
+                    for m in range(OUT_BLOCKS):
+                        nc.tensor.matmul(
+                            sums[m, c, h][:],
+                            weights[:, b, m * P : (m + 1) * P],
+                            x[:],
+                            start=b == 0,
+                            stop=b == BLOCKS - 1,
+                        )
 
                 if b == BLOCKS - 1:
-                    for m in range(OUT_BLOCKS):
-                        result = held.tile([P, PIECE], F32, name=f"result{m}{c}")
-                        if m == 0:
-                            nc.vector.tensor_copy(result[:], sums[m, c][:])
-                        else:
-                            nc.scalar.copy(result[:], sums[m, c][:])
-                        nc.sync.dma_start(out[m * P : (m + 1) * P, c * PIECE : (c + 1) * PIECE], result[:])
+                    for h in range(PARTS):
+                        first = c * PIECE + h * PART
+                        for m in range(OUT_BLOCKS):
+                            result = held.tile([P, PART], F32, name=f"result{m}{c}{h}")
+                            if c == PIECES - 1 and m == 0:
+                                nc.vector.tensor_copy(result[:], sums[m, c, h][:])
+                            else:
+                                nc.scalar.copy(result[:], sums[m, c, h][:])
+                            nc.sync.dma_start(out[m * P : (m + 1) * P, first : first + PART], result[:])

import concourse.mybir as mybir

BF16, F32, U16 = mybir.dt.bfloat16, mybir.dt.float32, mybir.dt.uint16
MULT = mybir.AluOpType.mult
SQUARE = mybir.ActivationFunctionType.Square

P = 128
K, S, N, M = 256, 2048, 1024, 256
BLOCKS = K // P
OUT_BLOCKS = M // P
PIECE = 512
PIECES = N // PIECE
PART = PIECE // 2
PARTS = PIECE // PART

FLOPS = 2 * K * M * N


def tile_lookup_gate_sq_none_kernel(tc, tab, y, w, offs, out):
    nc = tc.nc
    with (
        tc.tile_pool(name="held", bufs=1) as held,
        tc.psum_pool(name="psum", bufs=1) as psum,
    ):
        early_in = held.tile([P, 1], F32, name="early_in")
        nc.vector.memset(early_in[:], 0.0)
        early_out = held.tile([P, 1], F32, name="early_out")
        nc.scalar.activation(early_out[:], early_in[:], SQUARE)

        lists = held.tile([P, N // 16], U16, name="lists")
        weights = held.tile([P, BLOCKS, M], BF16, name="weights")
        tables, streams = {}, {}
        for b in range(BLOCKS):
            tables[b] = held.tile([P, S], F32, name=f"table{b}")
            for c in range(PIECES):
                streams[b, c] = held.tile([P, PIECE], F32, name=f"stream{b}{c}")

        def load_table(b):
            nc.sync.dma_start(tables[b][:], tab[b * P : (b + 1) * P, :])

        def load_stream(b, c):
            nc.sync.dma_start(streams[b, c][:], y[b * P : (b + 1) * P, c * PIECE : (c + 1) * PIECE])

        load_table(0)
        nc.sync.dma_start(lists[:], offs)
        nc.sync.dma_start(weights[:], w.rearrange("(b p) m -> p b m", p=P))
        load_stream(0, 0)
        load_table(1)
        load_stream(0, 1)
        load_stream(1, 0)
        load_stream(1, 1)

        squares = {}
        for b in range(BLOCKS):
            for c in range(PIECES):
                squares[b, c] = held.tile([P, PIECE], F32, name=f"square{b}{c}")
                piece = lists[:, c * PIECE // 16 : (c + 1) * PIECE // 16]
                nc.scalar.activation(squares[b, c][:], tables[b][:].indirect(piece), SQUARE)

        sums = {
            (m, c, h): psum.tile([P, PART], F32, name=f"sum{m}{c}{h}")
            for m in range(OUT_BLOCKS)
            for c in range(PIECES)
            for h in range(PARTS)
        }

        for b in range(BLOCKS):
            for c in range(PIECES):
                for h in range(PARTS):
                    part = slice(h * PART, (h + 1) * PART)
                    x = held.tile([P, PART], BF16, name=f"x{b}{c}{h}")
                    nc.vector.tensor_tensor(x[:], squares[b, c][:, part], streams[b, c][:, part], MULT)

                    for m in range(OUT_BLOCKS):
                        nc.tensor.matmul(
                            sums[m, c, h][:],
                            weights[:, b, m * P : (m + 1) * P],
                            x[:],
                            start=b == 0,
                            stop=b == BLOCKS - 1,
                        )

                if b == BLOCKS - 1:
                    for h in range(PARTS):
                        first = c * PIECE + h * PART
                        for m in range(OUT_BLOCKS):
                            result = held.tile([P, PART], F32, name=f"result{m}{c}{h}")
                            if c == PIECES - 1 and m == 0:
                                nc.vector.tensor_copy(result[:], sums[m, c, h][:])
                            else:
                                nc.scalar.copy(result[:], sums[m, c, h][:])
                            nc.sync.dma_start(out[m * P : (m + 1) * P, first : first + PART], result[:])
